import numpy as np
import ml_dtypes


def mxq(x, axis, fmt="e4m3"):
    dtype, down = {"e4m3": (ml_dtypes.float8_e4m3fn, 7), "e5m2": (ml_dtypes.float8_e5m2, 14)}[fmt]
    v = np.moveaxis(np.asarray(x, np.float32).astype(ml_dtypes.bfloat16).astype(np.float64), axis, -1)
    blocks = v.reshape(v.shape[:-1] + (-1, 32))
    amax = np.abs(blocks).max(-1, keepdims=True)
    byte = np.maximum(np.where(amax > 0, np.frexp(amax)[1] - 1 + 127, 0) - down, 1)
    scale = np.exp2(byte - 127.0)
    codes = (blocks / scale).astype(np.float32).astype(dtype).astype(np.float64)
    return np.moveaxis((codes * scale).reshape(v.shape), -1, axis)


WIDE = False


def mx_kscale(k):
    if not WIDE:
        return np.ones(k)
    levels = np.array([10, -10, 5, -5, 0])
    if k % 512:
        return np.exp2(np.random.permutation(np.resize(levels, k // 32))).repeat(32)
    a = np.empty((k // 512, 16))
    for p in range(k // 512):
        a[p, :8] = np.random.permutation(np.resize(levels, 8))
        for g in range(8):
            far = levels[np.abs(levels - a[p, g]) >= 10]
            a[p, g + 8] = far[np.random.randint(len(far))]
    return np.exp2(a.ravel()).repeat(32)


def f64(x):
    return np.asarray(x).astype(np.float64)


def striped(idx):
    return np.tile(idx.reshape(-1, 16).T, (8, 1)).astype(np.uint16)


def unstriped(offs):
    return offs[:16].T.reshape(-1).astype(np.int64)


def striped8(idx):
    return np.concatenate([x.reshape(-1, 16).T for x in idx]).astype(np.uint16)


def runs(offs, k):
    lists = np.stack([offs[16 * r : 16 * r + 16].T.reshape(-1) for r in range(8)]).astype(np.int64)
    return lists[np.arange(k) % 512 // 64]


def pack_weight(w):
    k, n = w.shape
    w = f64(np.asarray(w, np.float32).astype(ml_dtypes.bfloat16)).reshape(k // 32, 32, n)
    amax = np.abs(w).max(1)
    byte = np.clip(np.where(amax > 0, np.frexp(amax)[1] - 1 + 127 - 7, 1), 1, 254)
    scaled = (w * np.exp2(127.0 - byte)[:, None, :]).reshape(k, n).astype(np.float32)
    words = np.ascontiguousarray(scaled.reshape(k // 512, 128, 4, n).transpose(0, 1, 3, 2)).astype(ml_dtypes.float8_e4m3fn).view(np.uint8)
    return words, np.ascontiguousarray(byte.astype(np.uint8).reshape(k // 512, 16, n))


def unpack_weight(words, scales):
    g, p, n, _ = words.shape
    vals = np.ascontiguousarray(words).view(ml_dtypes.float8_e4m3fn).astype(np.float64) * np.repeat(np.exp2(scales.astype(np.float64) - 127.0), 8, axis=1)[..., None]
    return vals.transpose(0, 1, 3, 2).reshape(g * 512, n)

def planes(y):
    n, m = y.shape
    v = y.astype(np.float32).astype(ml_dtypes.bfloat16).astype(np.float64).reshape(n // 32, 32, m)
    top = np.abs(v).max(1)
    byte = np.clip(np.where(top > 0, np.frexp(top)[1] - 1 + 127 - 7, 1), 1, 254)
    codes = (v * np.exp2(127.0 - byte)[:, None, :]).reshape(n, m).astype(np.float32).astype(ml_dtypes.float8_e4m3fn).view(np.uint8)
    words = codes.reshape(n // 512, 128, 4, m).transpose(0, 1, 3, 2)
    return np.ascontiguousarray(words), np.ascontiguousarray(byte.astype(np.uint8).reshape(n // 512, 16, m))


K, T, S, N, G, H, W = 512, 2048, 512, 512, 2048, 512, 256


def setup_inputs():
    n = np.random.standard_normal
    s = mx_kscale(K)[:, None]
    u = mx_kscale(S)
    packed_xT = pack_weight(n((K, T)) * s)
    packed_dT = pack_weight(n((K, G)) / s)
    packed_w1 = pack_weight(n((H, N)) / np.sqrt(H) / u[:, None])
    perm = np.stack([np.random.permutation(S) for _ in range(8)])
    return {
        "x_words": packed_xT[0],
        "x_scales": packed_xT[1],
        "d_words": packed_dT[0],
        "d_scales": packed_dT[1],
        "gn": (np.random.uniform(0.5, 1.5, (H, 1)) * u[:, None]).astype(np.float32),
        "w1_words": packed_w1[0],
        "w1_scales": packed_w1[1],
        "offs": striped(np.random.permutation(T)[:S]),
        "k1": striped8(np.random.randint(0, G, (8, H))),
        "n1": striped8(np.stack([np.random.permutation(S) for _ in range(8)])),
        "n2": striped8(np.stack([np.random.permutation(S) for _ in range(8)])),
        "n3": striped8(perm[:, :W]),
        "n4": striped8(perm[:, W:]),
    }


def reference(x_words, x_scales, d_words, d_scales, gn, w1_words, w1_scales, offs, k1, n1, n2, n3, n4):
    d_k1 = unpack_weight(d_words, d_scales)[np.arange(K)[:, None], runs(k1, K)]
    xq = unpack_weight(x_words, x_scales)[:, unstriped(offs)]
    h = 0.0625 * (d_k1.T @ xq)
    ex = np.exp(h)
    z = f64(gn) * (np.log(ex + ex[np.arange(H)[:, None], runs(n1, H)]) - (h[np.arange(H)[:, None], runs(n2, H)]))
    h2 = unpack_weight(w1_words, w1_scales).T @ mxq(z, 0, "e4m3")
    pa = h2[np.arange(N)[:, None], runs(n3, N)]
    pb = h2[np.arange(N)[:, None], runs(n4, N)]
    ra = np.maximum(pa, pb)
    out = h2.copy()
    out[np.arange(N)[:, None], runs(n3, N)] = ra
    return (out,) + planes(out)

@@ -1,0 +1,207 @@
+from contextlib import ExitStack
+
+import concourse.mybir as mybir
+
+K, T, S, N, G, H, W = 512, 2048, 512, 512, 2048, 512, 256
+FLOPS = 2 * K * H * S + 2 * H * N * S
+
+F32 = mybir.dt.float32
+BF16 = mybir.dt.bfloat16
+I32 = mybir.dt.int32
+U32 = mybir.dt.uint32
+U16 = mybir.dt.uint16
+U8 = mybir.dt.uint8
+FP8X4 = mybir.dt.float8_e4m3fn_x4
+ALU = mybir.AluOpType
+ACT = mybir.ActivationFunctionType
+
+P = 128
+PACK = 4
+HALF = S // 2
+LCOLS = HALF // 16
+
+
+def words_view(dram):
+    return dram[0].rearrange("p n t -> p (n t)").bitcast(I32)
+
+
+def tile_picked_pqlaylsefill_none_po_kernel(tc, x_words, x_scales, d_words, d_scales, gn, w1_words, w1_scales, offs, k1, n1, n2, n3, n4, out_0, out_1, out_2):
+    nc = tc.nc
+    with ExitStack() as ctx:
+        keep = ctx.enter_context(tc.tile_pool(name="keep", bufs=1))
+        psum = ctx.enter_context(tc.psum_pool(name="psum", bufs=8))
+
+        def sb(name, shape, dtype):
+            return keep.tile(shape, dtype, name=name, align_bytes=64)
+
+        def load_list(name, dram):
+            t = sb(name, list(dram.shape), U16)
+            nc.sync.dma_start(t[:], dram)
+            return t
+
+        def deal(out, in_):
+            nc.vector.tensor_copy(out.rearrange("p (t m) -> p m t", t=PACK), in_.rearrange("p (m t) -> p m t", t=PACK))
+
+        def load_scale_rows(name, dram):
+            t = sb(name, [P, dram.shape[2]], U8)
+            rows = dram[0].bitcast(I32).rearrange("(u e) c -> e u c", e=2)
+            for e in range(2):
+                nc.sync.dma_start(t[e:P:2, :].bitcast(I32), rows[e].unsqueeze(1).to_broadcast([8, 8, dram.shape[2] // 4]))
+            return t
+
+        k1_t = load_list("k1_t", k1)
+        d_sc = load_scale_rows("d_sc", d_scales)
+        offs_t = load_list("offs_t", offs)
+        x_sc = load_scale_rows("x_sc", x_scales)
+        d_w = keep.tile([P, G], U32, name="d_w", tag="d_w", align_bytes=64)
+        nc.sync.dma_start(d_w[:].bitcast(I32), words_view(d_words))
+        x_w = sb("x_w", [P, T], U32)
+        nc.sync.dma_start(x_w[:].bitcast(I32), words_view(x_words))
+        w_w = sb("w_w", [P, N], U32)
+        nc.sync.dma_start(w_w[:].bitcast(I32), words_view(w1_words))
+        n1_t = load_list("n1_t", n1)
+        n2_t = load_list("n2_t", n2)
+        n3_t = load_list("n3_t", n3)
+        n4_t = load_list("n4_t", n4)
+        gain = sb("gain", [P, PACK], F32)
+        nc.gpsimd.dma_start(gain[:], gn.rearrange("(p t) o -> p (t o)", t=PACK))
+        gain16 = sb("gain16", [P, PACK], F32)
+        nc.gpsimd.tensor_scalar(gain16[:], gain[:], 0.0625, 0.0, ALU.mult, ALU.add)
+
+        d_sc_g = sb("d_sc_g", [P, H], U8)
+        nc.vector.tensor_copy(d_sc_g[:], d_sc[:].indirect(k1_t[:]))
+        x_sc_g = sb("x_sc_g", [P, S], U8)
+        nc.vector.tensor_copy(x_sc_g[:], x_sc[:].indirect(offs_t[:]))
+        sc1 = sb("sc1", [P, H + S], U8)
+        deal(sc1[:, :H], d_sc_g[:])
+        nc.vector.tensor_copy(sc1[:, H:].bitcast(I32), x_sc_g[:].bitcast(I32))
+        for e in range(2):
+            nc.scalar.dma_start(sc1[2 + e : P : 32, :].bitcast(I32), sc1[16 + e : P : 32, :].bitcast(I32))
+        d_w_g = sb("d_w_g", [P, H], U32)
+        nc.vector.tensor_copy(d_w_g[:], d_w[:].indirect(k1_t[:]))
+        d_w_d = sb("d_w_d", [P, H], U32)
+        deal(d_w_d[:].bitcast(I32), d_w_g[:].bitcast(I32))
+        x_w_g = sb("x_w_g", [P, S], U32)
+        nc.vector.tensor_copy(x_w_g[:], x_w[:].indirect(offs_t[:]))
+        w_sc = keep.tile([P, N], U8, name="w_sc", tag="d_w", align_bytes=64)
+        w_rows = w1_scales[0].bitcast(I32).rearrange("(q j) c -> j q c", j=4)
+        for j in range(4):
+            nc.sync.dma_start(w_sc[j:P:4, :].bitcast(I32), w_rows[j].unsqueeze(1).to_broadcast([4, 8, N // 4]))
+        w_w_d = sb("w_w_d", [P, N], U32)
+        deal(w_w_d[:].bitcast(I32), w_w[:].bitcast(I32))
+        w_sc_d = sb("w_sc_d", [P, N], U8)
+        deal(w_sc_d[:], w_sc[:])
+
+        acc = []
+        ex = []
+        for t in range(PACK):
+            cols = slice(P * t, P * (t + 1))
+            a = psum.tile([P, S], F32, name="acc", tag="acc")
+            nc.tensor.matmul_mx(out=a[:], lhsT=d_w_d[:, cols].bitcast(FP8X4), lhsT_scale=sc1[:, cols],
+                                rhs=x_w_g[:].bitcast(FP8X4), rhs_scale=sc1[:, H:], start=True, stop=True)
+            acc.append(a)
+        for t in range(PACK):
+            e = sb("ex%d" % t, [P, S], F32)
+            nc.scalar.activation(e[:], acc[t][:], ACT.Exp, scale=0.0625)
+            ex.append(e)
+
+        halves = [slice(HALF * u, HALF * (u + 1)) for u in range(2)]
+        lhalves = [slice(LCOLS * u, LCOLS * (u + 1)) for u in range(2)]
+        e1 = [sb("e1_%d" % u, [P, PACK, HALF], F32) for u in range(2)]
+        ssum = [sb("ssum%d" % u, [P, PACK, HALF], F32) for u in range(2)]
+        lse = [sb("lse%d" % u, [P, PACK, HALF], F32) for u in range(2)]
+        gh2 = [sb("gh2_%d" % u, [P, PACK, HALF], F32) for u in range(2)]
+        zb = [sb("zb%d" % u, [P, PACK, HALF], BF16) for u in range(2)]
+        gh = [sb("gh%d" % t, [P, S], F32) for t in range(PACK)]
+
+        z_w = [sb("z_w%d" % u, [P, HALF], U32) for u in range(2)]
+        z_sc = [sb("z_sc%d" % u, [P, HALF], U8) for u in range(2)]
+        h2 = [sb("h2_%d" % t, [P, S], F32) for t in range(PACK)]
+
+        def pair_sums(u):
+            for t in range(PACK + 1):
+                if t < PACK:
+                    nc.vector.tensor_copy(e1[u][:, t, :], ex[t][:].indirect(n1_t[:, lhalves[u]]))
+                if t > 0:
+                    nc.vector.tensor_tensor(ssum[u][:, t - 1, :], ex[t - 1][:, halves[u]], e1[u][:, t - 1, :], ALU.add)
+
+        def logs(u):
+            for t in range(PACK):
+                nc.scalar.activation(lse[u][:, t, :], ssum[u][:, t, :], ACT.Ln)
+
+        def fetch(u, t, on_vector):
+            window = gh[t][:].indirect(n2_t[:, lhalves[u]])
+            if on_vector:
+                nc.vector.tensor_copy(gh2[u][:, t, :], window)
+            else:
+                nc.scalar.activation(gh2[u][:, t, :], window, ACT.Copy)
+
+        def combine(u, t):
+            nc.vector.scalar_tensor_tensor(zb[u][:, t, :], lse[u][:, t, :], gain[:, t : t + 1], gh2[u][:, t, :], ALU.mult, ALU.subtract)
+
+        def quantise_z(u):
+            zi = sb("zi%d" % u, [P, HALF, PACK], BF16)
+            nc.vector.tensor_copy(zi[:].rearrange("p (c i) t -> p c t i", i=4), zb[u][:].rearrange("p t (c i) -> p c t i", i=4))
+            nc.vector.quantize_mx(out=z_w[u][:].bitcast(FP8X4), scales=z_sc[u][:], in_=zi[:].rearrange("p c t -> p (c t)"))
+
+        def second_product(u):
+            for t in range(PACK):
+                cols = slice(P * t, P * (t + 1))
+                a = psum.tile([P, HALF], F32, name="acc2", tag="acc")
+                nc.tensor.matmul_mx(out=a[:], lhsT=w_w_d[:, cols].bitcast(FP8X4), lhsT_scale=w_sc_d[:, cols],
+                                    rhs=z_w[u][:].bitcast(FP8X4), rhs_scale=z_sc[u][:], start=True, stop=True)
+                nc.scalar.copy(h2[t][:, halves[u]], a[:])
+
+        for t in range(2):
+            nc.scalar.activation(gh[t][:], acc[t][:], ACT.Copy, scale=gain16[:, t : t + 1])
+        pair_sums(0)
+        logs(0)
+        for t in range(2, PACK):
+            nc.vector.tensor_scalar(gh[t][:], acc[t][:], gain16[:, t : t + 1], None, ALU.mult)
+        for t in range(PACK):
+            fetch(0, t, False)
+        pair_sums(1)
+        logs(1)
+        for t in range(PACK - 1):
+            fetch(1, t, False)
+        for t in range(PACK):
+            combine(0, t)
+        quantise_z(0)
+        fetch(1, PACK - 1, True)
+        for t in range(PACK):
+            combine(1, t)
+        quantise_z(1)
+        second_product(0)
+        second_product(1)
+
+        out_rows = out_0.rearrange("(p t) c -> t p c", t=PACK)
+        yb = [sb("yb%d" % u, [P, PACK, HALF], BF16) for u in range(2)]
+        for t in range(PACK):
+            pa = sb("pa%d" % t, [P, W], F32)
+            pb = sb("pb%d" % t, [P, W], F32)
+            ra = sb("ra%d" % t, [P, W], F32)
+            nc.scalar.activation(pa[:], h2[t][:].indirect(n3_t[:]), ACT.Copy)
+            if t == 0:
+                nc.vector.tensor_copy(pb[:], h2[t][:].indirect(n4_t[:]))
+            else:
+                nc.scalar.activation(pb[:], h2[t][:].indirect(n4_t[:]), ACT.Copy)
+            nc.vector.tensor_tensor(ra[:], pa[:], pb[:], ALU.max)
+            nc.vector.tensor_copy(h2[t][:].indirect(n3_t[:]), ra[:])
+            nc.sync.dma_start(out_rows[t], h2[t][:])
+        for t in range(PACK):
+            for u in range(2):
+                if t == PACK - 1 and u == 0:
+                    nc.vector.tensor_copy(yb[u][:, t, :], h2[t][:, halves[u]])
+                else:
+                    nc.scalar.copy(yb[u][:, t, :], h2[t][:, halves[u]])
+        y_w = sb("y_w", [P, S], U32)
+        y_sc = sb("y_sc", [P, S], U8)
+        out_w = words_view(out_1)
+        for u in range(2):
+            yi = sb("yi%d" % u, [P, HALF, PACK], BF16)
+            nc.vector.tensor_copy(yi[:].rearrange("p (c i) t -> p c t i", i=4), yb[u][:].rearrange("p t (c i) -> p c t i", i=4))
+            nc.vector.quantize_mx(out=y_w[:, halves[u]].bitcast(FP8X4), scales=y_sc[:, halves[u]], in_=yi[:].rearrange("p c t -> p (c t)"))
+            nc.sync.dma_start(out_w[:, halves[u]], y_w[:, halves[u]].bitcast(I32))
+        for q in range(4):
+            eng = nc.scalar if q % 2 else nc.sync
+            eng.dma_start(out_2[0][4 * q : 4 * q + 4, :].bitcast(I32), y_sc[32 * q : 32 * q + 4, :].bitcast(I32))

@@ -29,6 +29,7 @@ def tile_picked_pqlaylsefill_none_po_kernel(tc, x_words, x_scales, d_words, d_sc
     nc = tc.nc
     with ExitStack() as ctx:
         keep = ctx.enter_context(tc.tile_pool(name="keep", bufs=1))
+        shared = ctx.enter_context(tc.tile_pool(name="shared", bufs=1))
         psum = ctx.enter_context(tc.psum_pool(name="psum", bufs=8))
 
         def sb(name, shape, dtype):
@@ -42,23 +43,21 @@ def tile_picked_pqlaylsefill_none_po_kernel(tc, x_words, x_scales, d_words, d_sc
         def deal(out, in_):
             nc.vector.tensor_copy(out.rearrange("p (t m) -> p m t", t=PACK), in_.rearrange("p (m t) -> p m t", t=PACK))
 
+        halves = [slice(HALF * u, HALF * (u + 1)) for u in range(2)]
+        lhalves = [slice(LCOLS * u, LCOLS * (u + 1)) for u in range(2)]
         def load_scale_rows(name, dram):
             t = sb(name, [P, dram.shape[2]], U8)
-            rows = dram[0].bitcast(I32).rearrange("(u e) c -> e u c", e=2)
-            for e in range(2):
-                nc.sync.dma_start(t[e:P:2, :].bitcast(I32), rows[e].unsqueeze(1).to_broadcast([8, 8, dram.shape[2] // 4]))
+            nc.sync.dma_start(t[:].bitcast(I32), dram[0].bitcast(I32).unsqueeze(1).to_broadcast([16, 8, dram.shape[2] // 4]))
             return t
 
         k1_t = load_list("k1_t", k1)
         d_sc = load_scale_rows("d_sc", d_scales)
         offs_t = load_list("offs_t", offs)
         x_sc = load_scale_rows("x_sc", x_scales)
-        d_w = keep.tile([P, G], U32, name="d_w", tag="d_w", align_bytes=64)
+        d_w = shared.tile([P, G], U32, name="d_w", offset=0, align_bytes=64)
         nc.sync.dma_start(d_w[:].bitcast(I32), words_view(d_words))
         x_w = sb("x_w", [P, T], U32)
         nc.sync.dma_start(x_w[:].bitcast(I32), words_view(x_words))
-        w_w = sb("w_w", [P, N], U32)
-        nc.sync.dma_start(w_w[:].bitcast(I32), words_view(w1_words))
         n1_t = load_list("n1_t", n1)
         n2_t = load_list("n2_t", n2)
         n3_t = load_list("n3_t", n3)
@@ -75,15 +74,18 @@ def tile_picked_pqlaylsefill_none_po_kernel(tc, x_words, x_scales, d_words, d_sc
         sc1 = sb("sc1", [P, H + S], U8)
         deal(sc1[:, :H], d_sc_g[:])
         nc.vector.tensor_copy(sc1[:, H:].bitcast(I32), x_sc_g[:].bitcast(I32))
-        for e in range(2):
-            nc.scalar.dma_start(sc1[2 + e : P : 32, :].bitcast(I32), sc1[16 + e : P : 32, :].bitcast(I32))
+        for j in range(1, 4):
+            nc.scalar.dma_start(sc1[j:P:32, :].bitcast(I32), sc1[8 * j : P : 32, :].bitcast(I32))
         d_w_g = sb("d_w_g", [P, H], U32)
         nc.vector.tensor_copy(d_w_g[:], d_w[:].indirect(k1_t[:]))
         d_w_d = sb("d_w_d", [P, H], U32)
         deal(d_w_d[:].bitcast(I32), d_w_g[:].bitcast(I32))
         x_w_g = sb("x_w_g", [P, S], U32)
-        nc.vector.tensor_copy(x_w_g[:], x_w[:].indirect(offs_t[:]))
-        w_sc = keep.tile([P, N], U8, name="w_sc", tag="d_w", align_bytes=64)
+        for u in range(2):
+            nc.vector.tensor_copy(x_w_g[:, halves[u]], x_w[:].indirect(offs_t[:, lhalves[u]]))
+        w_w = shared.tile([P, N], U32, name="w_w", offset=0, align_bytes=64)
+        nc.sync.dma_start(w_w[:].bitcast(I32), words_view(w1_words))
+        w_sc = shared.tile([P, N], U8, name="w_sc", offset=4 * N, align_bytes=64)
         w_rows = w1_scales[0].bitcast(I32).rearrange("(q j) c -> j q c", j=4)
         for j in range(4):
             nc.sync.dma_start(w_sc[j:P:4, :].bitcast(I32), w_rows[j].unsqueeze(1).to_broadcast([4, 8, N // 4]))
@@ -92,21 +94,17 @@ def tile_picked_pqlaylsefill_none_po_kernel(tc, x_words, x_scales, d_words, d_sc
         w_sc_d = sb("w_sc_d", [P, N], U8)
         deal(w_sc_d[:], w_sc[:])
 
+        ex = [sb("ex%d" % t, [P, S], F32) for t in range(PACK)]
+        pieces = [(0, halves[0]), (0, halves[1])] + [(t, slice(0, S)) for t in range(1, PACK)]
         acc = []
-        ex = []
-        for t in range(PACK):
+        for t, js in pieces:
             cols = slice(P * t, P * (t + 1))
-            a = psum.tile([P, S], F32, name="acc", tag="acc")
+            a = psum.tile([P, js.stop - js.start], F32, name="acc", tag="acc")
             nc.tensor.matmul_mx(out=a[:], lhsT=d_w_d[:, cols].bitcast(FP8X4), lhsT_scale=sc1[:, cols],
-                                rhs=x_w_g[:].bitcast(FP8X4), rhs_scale=sc1[:, H:], start=True, stop=True)
+                                rhs=x_w_g[:, js].bitcast(FP8X4), rhs_scale=sc1[:, H + js.start : H + js.stop], start=True, stop=True)
+            nc.scalar.activation(ex[t][:, js], a[:], ACT.Exp, scale=0.0625)
             acc.append(a)
-        for t in range(PACK):
-            e = sb("ex%d" % t, [P, S], F32)
-            nc.scalar.activation(e[:], acc[t][:], ACT.Exp, scale=0.0625)
-            ex.append(e)
 
-        halves = [slice(HALF * u, HALF * (u + 1)) for u in range(2)]
-        lhalves = [slice(LCOLS * u, LCOLS * (u + 1)) for u in range(2)]
         e1 = [sb("e1_%d" % u, [P, PACK, HALF], F32) for u in range(2)]
         ssum = [sb("ssum%d" % u, [P, PACK, HALF], F32) for u in range(2)]
         lse = [sb("lse%d" % u, [P, PACK, HALF], F32) for u in range(2)]
@@ -114,8 +112,10 @@ def tile_picked_pqlaylsefill_none_po_kernel(tc, x_words, x_scales, d_words, d_sc
         zb = [sb("zb%d" % u, [P, PACK, HALF], BF16) for u in range(2)]
         gh = [sb("gh%d" % t, [P, S], F32) for t in range(PACK)]
 
-        z_w = [sb("z_w%d" % u, [P, HALF], U32) for u in range(2)]
-        z_sc = [sb("z_sc%d" % u, [P, HALF], U8) for u in range(2)]
+        chunks = [(0, 0, HALF), (1, 0, HALF // 2), (1, HALF // 2, HALF)]
+        z_w = [sb("z_w%d" % i, [P, hi - lo], U32) for i, (u, lo, hi) in enumerate(chunks)]
+        z_sc = [sb("z_sc%d" % i, [P, hi - lo], U8) for i, (u, lo, hi) in enumerate(chunks)]
+        zi = [sb("zi%d" % i, [P, hi - lo, PACK], BF16) for i, (u, lo, hi) in enumerate(chunks)]
         h2 = [sb("h2_%d" % t, [P, S], F32) for t in range(PACK)]
 
         def pair_sums(u):
@@ -139,25 +139,29 @@ def tile_picked_pqlaylsefill_none_po_kernel(tc, x_words, x_scales, d_words, d_sc
         def combine(u, t):
             nc.vector.scalar_tensor_tensor(zb[u][:, t, :], lse[u][:, t, :], gain[:, t : t + 1], gh2[u][:, t, :], ALU.mult, ALU.subtract)
 
-        def quantise_z(u):
-            zi = sb("zi%d" % u, [P, HALF, PACK], BF16)
-            nc.vector.tensor_copy(zi[:].rearrange("p (c i) t -> p c t i", i=4), zb[u][:].rearrange("p t (c i) -> p c t i", i=4))
-            nc.vector.quantize_mx(out=z_w[u][:].bitcast(FP8X4), scales=z_sc[u][:], in_=zi[:].rearrange("p c t -> p (c t)"))
+        def mover(on_vector):
+            return nc.vector.tensor_copy if on_vector else nc.scalar.copy
 
-        def second_product(u):
-            for t in range(PACK):
-                cols = slice(P * t, P * (t + 1))
-                a = psum.tile([P, HALF], F32, name="acc2", tag="acc")
-                nc.tensor.matmul_mx(out=a[:], lhsT=w_w_d[:, cols].bitcast(FP8X4), lhsT_scale=w_sc_d[:, cols],
-                                    rhs=z_w[u][:].bitcast(FP8X4), rhs_scale=z_sc[u][:], start=True, stop=True)
-                nc.scalar.copy(h2[t][:, halves[u]], a[:])
+        def interleave_z(i):
+            u, lo, hi = chunks[i]
+            nc.vector.tensor_copy(zi[i][:].rearrange("p (c i) t -> p c t i", i=4), zb[u][:, :, lo:hi].rearrange("p t (c i) -> p c t i", i=4))
 
-        for t in range(2):
-            nc.scalar.activation(gh[t][:], acc[t][:], ACT.Copy, scale=gain16[:, t : t + 1])
+        def quantise_z(i):
+            nc.vector.quantize_mx(out=z_w[i][:].bitcast(FP8X4), scales=z_sc[i][:], in_=zi[i][:].rearrange("p c t -> p (c t)"))
+
+        def second_product(i, t, on_vector=False):
+            u, lo, hi = chunks[i]
+            cols = slice(P * t, P * (t + 1))
+            a = psum.tile([P, hi - lo], F32, name="acc2", tag="acc")
+            nc.tensor.matmul_mx(out=a[:], lhsT=w_w_d[:, cols].bitcast(FP8X4), lhsT_scale=w_sc_d[:, cols],
+                                rhs=z_w[i][:].bitcast(FP8X4), rhs_scale=z_sc[i][:], start=True, stop=True)
+            mover(on_vector)(h2[t][:, HALF * u + lo : HALF * u + hi], a[:])
+
+        for (t, js), a in list(zip(pieces, acc))[:4]:
+            nc.scalar.activation(gh[t][:, js], a[:], ACT.Copy, scale=gain16[:, t : t + 1])
         pair_sums(0)
         logs(0)
-        for t in range(2, PACK):
-            nc.vector.tensor_scalar(gh[t][:], acc[t][:], gain16[:, t : t + 1], None, ALU.mult)
+        nc.vector.tensor_scalar(gh[3][:], acc[4][:], gain16[:, 3:4], None, ALU.mult)
         for t in range(PACK):
             fetch(0, t, False)
         pair_sums(1)
@@ -166,41 +170,50 @@ def tile_picked_pqlaylsefill_none_po_kernel(tc, x_words, x_scales, d_words, d_sc
             fetch(1, t, False)
         for t in range(PACK):
             combine(0, t)
+        interleave_z(0)
         quantise_z(0)
         fetch(1, PACK - 1, True)
         for t in range(PACK):
             combine(1, t)
+        interleave_z(1)
+        interleave_z(2)
         quantise_z(1)
-        second_product(0)
-        second_product(1)
+        quantise_z(2)
+        for t in range(PACK):
+            second_product(0, t)
 
         out_rows = out_0.rearrange("(p t) c -> t p c", t=PACK)
-        yb = [sb("yb%d" % u, [P, PACK, HALF], BF16) for u in range(2)]
-        for t in range(PACK):
-            pa = sb("pa%d" % t, [P, W], F32)
-            pb = sb("pb%d" % t, [P, W], F32)
-            ra = sb("ra%d" % t, [P, W], F32)
-            nc.scalar.activation(pa[:], h2[t][:].indirect(n3_t[:]), ACT.Copy)
-            if t == 0:
-                nc.vector.tensor_copy(pb[:], h2[t][:].indirect(n4_t[:]))
-            else:
-                nc.scalar.activation(pb[:], h2[t][:].indirect(n4_t[:]), ACT.Copy)
-            nc.vector.tensor_tensor(ra[:], pa[:], pb[:], ALU.max)
-            nc.vector.tensor_copy(h2[t][:].indirect(n3_t[:]), ra[:])
-            nc.sync.dma_start(out_rows[t], h2[t][:])
-        for t in range(PACK):
-            for u in range(2):
-                if t == PACK - 1 and u == 0:
-                    nc.vector.tensor_copy(yb[u][:, t, :], h2[t][:, halves[u]])
+        yb = [[sb("yb%d_%d" % (r, u), [P, 2, HALF], BF16) for u in range(2)] for r in range(2)]
+        yi = [sb("yi%d" % u, [P, HALF, PACK], BF16) for u in range(2)]
+        for group in ([0], [1], [2, 3]):
+            pa = sb("pa%d" % group[0], [P, len(group), W], F32)
+            pb = sb("pb%d" % group[0], [P, len(group), W], F32)
+            ra = sb("ra%d" % group[0], [P, len(group), W], F32)
+            for t in group:
+                second_product(1, t)
+                second_product(2, t, t == 0)
+            for i, t in enumerate(group):
+                nc.scalar.activation(pa[:, i, :], h2[t][:].indirect(n3_t[:]), ACT.Copy)
+                if t == 0:
+                    nc.vector.tensor_copy(pb[:, i, :], h2[t][:].indirect(n4_t[:]))
                 else:
-                    nc.scalar.copy(yb[u][:, t, :], h2[t][:, halves[u]])
+                    nc.scalar.activation(pb[:, i, :], h2[t][:].indirect(n4_t[:]), ACT.Copy)
+            nc.vector.tensor_tensor(ra[:], pa[:], pb[:], ALU.max)
+            for i, t in enumerate(group):
+                nc.vector.tensor_copy(h2[t][:].indirect(n3_t[:]), ra[:, i, :])
+                nc.sync.dma_start(out_rows[t], h2[t][:])
+
         y_w = sb("y_w", [P, S], U32)
         y_sc = sb("y_sc", [P, S], U8)
         out_w = words_view(out_1)
+        for r in range(2):
+            for e in range(2):
+                for u in range(2):
+                    mover(r == 1 and e == 1 and u == 0)(yb[r][u][:, e, :], h2[2 * r + e][:, halves[u]])
+            for u in range(2):
+                mover(r == 1 and u == 0)(yi[u][:, :, 2 * r : 2 * r + 2], yb[r][u][:].rearrange("p e c -> p c e"))
         for u in range(2):
-            yi = sb("yi%d" % u, [P, HALF, PACK], BF16)
-            nc.vector.tensor_copy(yi[:].rearrange("p (c i) t -> p c t i", i=4), yb[u][:].rearrange("p t (c i) -> p c t i", i=4))
-            nc.vector.quantize_mx(out=y_w[:, halves[u]].bitcast(FP8X4), scales=y_sc[:, halves[u]], in_=yi[:].rearrange("p c t -> p (c t)"))
+            nc.vector.quantize_mx(out=y_w[:, halves[u]].bitcast(FP8X4), scales=y_sc[:, halves[u]], in_=yi[u][:].rearrange("p c t -> p (c t)"))
             nc.sync.dma_start(out_w[:, halves[u]], y_w[:, halves[u]].bitcast(I32))
         for q in range(4):
             eng = nc.scalar if q % 2 else nc.sync

@@ -123,7 +123,7 @@ def tile_picked_pqlaylsefill_none_po_kernel(tc, x_words, x_scales, d_words, d_sc
                 if t < PACK:
                     nc.vector.tensor_copy(e1[u][:, t, :], ex[t][:].indirect(n1_t[:, lhalves[u]]))
                 if t > 0:
-                    nc.vector.tensor_tensor(ssum[u][:, t - 1, :], ex[t - 1][:, halves[u]], e1[u][:, t - 1, :], ALU.add)
+                    nc.gpsimd.tensor_tensor(ssum[u][:, t - 1, :], ex[t - 1][:, halves[u]], e1[u][:, t - 1, :], ALU.add)
 
         def logs(u):
             for t in range(PACK):
@@ -160,18 +160,21 @@ def tile_picked_pqlaylsefill_none_po_kernel(tc, x_words, x_scales, d_words, d_sc
         for (t, js), a in list(zip(pieces, acc))[:4]:
             nc.scalar.activation(gh[t][:, js], a[:], ACT.Copy, scale=gain16[:, t : t + 1])
         pair_sums(0)
+        for t in range(2):
+            fetch(0, t, False)
         logs(0)
         nc.vector.tensor_scalar(gh[3][:], acc[4][:], gain16[:, 3:4], None, ALU.mult)
-        for t in range(PACK):
-            fetch(0, t, False)
+        for t in range(2, PACK):
+            fetch(0, t, t == PACK - 1)
         pair_sums(1)
         logs(1)
-        for t in range(PACK - 1):
+        for t in range(PACK - 2):
             fetch(1, t, False)
         for t in range(PACK):
             combine(0, t)
         interleave_z(0)
         quantise_z(0)
+        fetch(1, PACK - 2, True)
         fetch(1, PACK - 1, True)
         for t in range(PACK):
             combine(1, t)

from contextlib import ExitStack

import concourse.mybir as mybir

K, T, S, N, G, H, W = 512, 2048, 512, 512, 2048, 512, 256
FLOPS = 2 * K * H * S + 2 * H * N * S

F32 = mybir.dt.float32
BF16 = mybir.dt.bfloat16
I32 = mybir.dt.int32
U32 = mybir.dt.uint32
U16 = mybir.dt.uint16
U8 = mybir.dt.uint8
FP8X4 = mybir.dt.float8_e4m3fn_x4
ALU = mybir.AluOpType
ACT = mybir.ActivationFunctionType

P = 128
PACK = 4
HALF = S // 2
LCOLS = HALF // 16


def words_view(dram):
    return dram[0].rearrange("p n t -> p (n t)").bitcast(I32)


def tile_picked_pqlaylsefill_none_po_kernel(tc, x_words, x_scales, d_words, d_scales, gn, w1_words, w1_scales, offs, k1, n1, n2, n3, n4, out_0, out_1, out_2):
    nc = tc.nc
    with ExitStack() as ctx:
        keep = ctx.enter_context(tc.tile_pool(name="keep", bufs=1))
        shared = ctx.enter_context(tc.tile_pool(name="shared", bufs=1))
        psum = ctx.enter_context(tc.psum_pool(name="psum", bufs=8))

        def sb(name, shape, dtype):
            return keep.tile(shape, dtype, name=name, align_bytes=64)

        def load_list(name, dram):
            t = sb(name, list(dram.shape), U16)
            nc.sync.dma_start(t[:], dram)
            return t

        def deal(out, in_):
            nc.vector.tensor_copy(out.rearrange("p (t m) -> p m t", t=PACK), in_.rearrange("p (m t) -> p m t", t=PACK))

        halves = [slice(HALF * u, HALF * (u + 1)) for u in range(2)]
        lhalves = [slice(LCOLS * u, LCOLS * (u + 1)) for u in range(2)]
        def load_scale_rows(name, dram):
            t = sb(name, [P, dram.shape[2]], U8)
            nc.sync.dma_start(t[:].bitcast(I32), dram[0].bitcast(I32).unsqueeze(1).to_broadcast([16, 8, dram.shape[2] // 4]))
            return t

        k1_t = load_list("k1_t", k1)
        d_sc = load_scale_rows("d_sc", d_scales)
        offs_t = load_list("offs_t", offs)
        x_sc = load_scale_rows("x_sc", x_scales)
        d_w = shared.tile([P, G], U32, name="d_w", offset=0, align_bytes=64)
        nc.sync.dma_start(d_w[:].bitcast(I32), words_view(d_words))
        x_w = sb("x_w", [P, T], U32)
        nc.sync.dma_start(x_w[:].bitcast(I32), words_view(x_words))
        n1_t = load_list("n1_t", n1)
        n2_t = load_list("n2_t", n2)
        n3_t = load_list("n3_t", n3)
        n4_t = load_list("n4_t", n4)
        gain = sb("gain", [P, PACK], F32)
        nc.gpsimd.dma_start(gain[:], gn.rearrange("(p t) o -> p (t o)", t=PACK))
        gain16 = sb("gain16", [P, PACK], F32)
        nc.gpsimd.tensor_scalar(gain16[:], gain[:], 0.0625, 0.0, ALU.mult, ALU.add)

        d_sc_g = sb("d_sc_g", [P, H], U8)
        nc.vector.tensor_copy(d_sc_g[:], d_sc[:].indirect(k1_t[:]))
        x_sc_g = sb("x_sc_g", [P, S], U8)
        nc.vector.tensor_copy(x_sc_g[:], x_sc[:].indirect(offs_t[:]))
        sc1 = sb("sc1", [P, H + S], U8)
        deal(sc1[:, :H], d_sc_g[:])
        nc.vector.tensor_copy(sc1[:, H:].bitcast(I32), x_sc_g[:].bitcast(I32))
        for j in range(1, 4):
            nc.scalar.dma_start(sc1[j:P:32, :].bitcast(I32), sc1[8 * j : P : 32, :].bitcast(I32))
        d_w_g = sb("d_w_g", [P, H], U32)
        nc.vector.tensor_copy(d_w_g[:], d_w[:].indirect(k1_t[:]))
        d_w_d = sb("d_w_d", [P, H], U32)
        deal(d_w_d[:].bitcast(I32), d_w_g[:].bitcast(I32))
        x_w_g = sb("x_w_g", [P, S], U32)
        for u in range(2):
            nc.vector.tensor_copy(x_w_g[:, halves[u]], x_w[:].indirect(offs_t[:, lhalves[u]]))
        w_w = shared.tile([P, N], U32, name="w_w", offset=0, align_bytes=64)
        nc.sync.dma_start(w_w[:].bitcast(I32), words_view(w1_words))
        w_sc = shared.tile([P, N], U8, name="w_sc", offset=4 * N, align_bytes=64)
        w_rows = w1_scales[0].bitcast(I32).rearrange("(q j) c -> j q c", j=4)
        for j in range(4):
            nc.sync.dma_start(w_sc[j:P:4, :].bitcast(I32), w_rows[j].unsqueeze(1).to_broadcast([4, 8, N // 4]))
        w_w_d = sb("w_w_d", [P, N], U32)
        deal(w_w_d[:].bitcast(I32), w_w[:].bitcast(I32))
        w_sc_d = sb("w_sc_d", [P, N], U8)
        deal(w_sc_d[:], w_sc[:])

        ex = [sb("ex%d" % t, [P, S], F32) for t in range(PACK)]
        pieces = [(0, halves[0]), (0, halves[1])] + [(t, slice(0, S)) for t in range(1, PACK)]
        acc = []
        for t, js in pieces:
            cols = slice(P * t, P * (t + 1))
            a = psum.tile([P, js.stop - js.start], F32, name="acc", tag="acc")
            nc.tensor.matmul_mx(out=a[:], lhsT=d_w_d[:, cols].bitcast(FP8X4), lhsT_scale=sc1[:, cols],
                                rhs=x_w_g[:, js].bitcast(FP8X4), rhs_scale=sc1[:, H + js.start : H + js.stop], start=True, stop=True)
            nc.scalar.activation(ex[t][:, js], a[:], ACT.Exp, scale=0.0625)
            acc.append(a)

        e1 = [sb("e1_%d" % u, [P, PACK, HALF], F32) for u in range(2)]
        ssum = [sb("ssum%d" % u, [P, PACK, HALF], F32) for u in range(2)]
        lse = [sb("lse%d" % u, [P, PACK, HALF], F32) for u in range(2)]
        gh2 = [sb("gh2_%d" % u, [P, PACK, HALF], F32) for u in range(2)]
        zb = [sb("zb%d" % u, [P, PACK, HALF], BF16) for u in range(2)]
        gh = [sb("gh%d" % t, [P, S], F32) for t in range(PACK)]

        chunks = [(0, 0, HALF), (1, 0, HALF // 2), (1, HALF // 2, HALF)]
        z_w = [sb("z_w%d" % i, [P, hi - lo], U32) for i, (u, lo, hi) in enumerate(chunks)]
        z_sc = [sb("z_sc%d" % i, [P, hi - lo], U8) for i, (u, lo, hi) in enumerate(chunks)]
        zi = [sb("zi%d" % i, [P, hi - lo, PACK], BF16) for i, (u, lo, hi) in enumerate(chunks)]
        h2 = [sb("h2_%d" % t, [P, S], F32) for t in range(PACK)]

        def pair_sums(u):
            for t in range(PACK + 1):
                if t < PACK:
                    nc.vector.tensor_copy(e1[u][:, t, :], ex[t][:].indirect(n1_t[:, lhalves[u]]))
                if t > 0:
                    nc.gpsimd.tensor_tensor(ssum[u][:, t - 1, :], ex[t - 1][:, halves[u]], e1[u][:, t - 1, :], ALU.add)

        def logs(u):
            for t in range(PACK):
                nc.scalar.activation(lse[u][:, t, :], ssum[u][:, t, :], ACT.Ln)

        def fetch(u, t, on_vector):
            window = gh[t][:].indirect(n2_t[:, lhalves[u]])
            if on_vector:
                nc.vector.tensor_copy(gh2[u][:, t, :], window)
            else:
                nc.scalar.activation(gh2[u][:, t, :], window, ACT.Copy)

        def combine(u, t):
            nc.vector.scalar_tensor_tensor(zb[u][:, t, :], lse[u][:, t, :], gain[:, t : t + 1], gh2[u][:, t, :], ALU.mult, ALU.subtract)

        def mover(on_vector):
            return nc.vector.tensor_copy if on_vector else nc.scalar.copy

        def interleave_z(i):
            u, lo, hi = chunks[i]
            nc.vector.tensor_copy(zi[i][:].rearrange("p (c i) t -> p c t i", i=4), zb[u][:, :, lo:hi].rearrange("p t (c i) -> p c t i", i=4))

        def quantise_z(i):
            nc.vector.quantize_mx(out=z_w[i][:].bitcast(FP8X4), scales=z_sc[i][:], in_=zi[i][:].rearrange("p c t -> p (c t)"))

        def second_product(i, t, on_vector=False):
            u, lo, hi = chunks[i]
            cols = slice(P * t, P * (t + 1))
            a = psum.tile([P, hi - lo], F32, name="acc2", tag="acc")
            nc.tensor.matmul_mx(out=a[:], lhsT=w_w_d[:, cols].bitcast(FP8X4), lhsT_scale=w_sc_d[:, cols],
                                rhs=z_w[i][:].bitcast(FP8X4), rhs_scale=z_sc[i][:], start=True, stop=True)
            mover(on_vector)(h2[t][:, HALF * u + lo : HALF * u + hi], a[:])

        for (t, js), a in list(zip(pieces, acc))[:4]:
            nc.scalar.activation(gh[t][:, js], a[:], ACT.Copy, scale=gain16[:, t : t + 1])
        pair_sums(0)
        for t in range(2):
            fetch(0, t, False)
        logs(0)
        nc.vector.tensor_scalar(gh[3][:], acc[4][:], gain16[:, 3:4], None, ALU.mult)
        for t in range(2, PACK):
            fetch(0, t, t == PACK - 1)
        pair_sums(1)
        logs(1)
        for t in range(PACK - 2):
            fetch(1, t, False)
        for t in range(PACK):
            combine(0, t)
        interleave_z(0)
        quantise_z(0)
        fetch(1, PACK - 2, True)
        fetch(1, PACK - 1, True)
        for t in range(PACK):
            combine(1, t)
        interleave_z(1)
        interleave_z(2)
        quantise_z(1)
        quantise_z(2)
        for t in range(PACK):
            second_product(0, t)

        out_rows = out_0.rearrange("(p t) c -> t p c", t=PACK)
        yb = [[sb("yb%d_%d" % (r, u), [P, 2, HALF], BF16) for u in range(2)] for r in range(2)]
        yi = [sb("yi%d" % u, [P, HALF, PACK], BF16) for u in range(2)]
        for group in ([0], [1], [2, 3]):
            pa = sb("pa%d" % group[0], [P, len(group), W], F32)
            pb = sb("pb%d" % group[0], [P, len(group), W], F32)
            ra = sb("ra%d" % group[0], [P, len(group), W], F32)
            for t in group:
                second_product(1, t)
                second_product(2, t, t == 0)
            for i, t in enumerate(group):
                nc.scalar.activation(pa[:, i, :], h2[t][:].indirect(n3_t[:]), ACT.Copy)
                if t == 0:
                    nc.vector.tensor_copy(pb[:, i, :], h2[t][:].indirect(n4_t[:]))
                else:
                    nc.scalar.activation(pb[:, i, :], h2[t][:].indirect(n4_t[:]), ACT.Copy)
            nc.vector.tensor_tensor(ra[:], pa[:], pb[:], ALU.max)
            for i, t in enumerate(group):
                nc.vector.tensor_copy(h2[t][:].indirect(n3_t[:]), ra[:, i, :])
                nc.sync.dma_start(out_rows[t], h2[t][:])

        y_w = sb("y_w", [P, S], U32)
        y_sc = sb("y_sc", [P, S], U8)
        out_w = words_view(out_1)
        for r in range(2):
            for e in range(2):
                for u in range(2):
                    mover(r == 1 and e == 1 and u == 0)(yb[r][u][:, e, :], h2[2 * r + e][:, halves[u]])
            for u in range(2):
                mover(r == 1 and u == 0)(yi[u][:, :, 2 * r : 2 * r + 2], yb[r][u][:].rearrange("p e c -> p c e"))
        for u in range(2):
            nc.vector.quantize_mx(out=y_w[:, halves[u]].bitcast(FP8X4), scales=y_sc[:, halves[u]], in_=yi[u][:].rearrange("p c t -> p (c t)"))
            nc.sync.dma_start(out_w[:, halves[u]], y_w[:, halves[u]].bitcast(I32))
        for q in range(4):
            eng = nc.scalar if q % 2 else nc.sync
            eng.dma_start(out_2[0][4 * q : 4 * q + 4, :].bitcast(I32), y_sc[32 * q : 32 * q + 4, :].bitcast(I32))
